import numpy as np
import ml_dtypes


def mxq(x, axis, fmt="e4m3"):
    dtype, down = {"e4m3": (ml_dtypes.float8_e4m3fn, 7), "e5m2": (ml_dtypes.float8_e5m2, 14)}[fmt]
    v = np.moveaxis(np.asarray(x, np.float32).astype(ml_dtypes.bfloat16).astype(np.float64), axis, -1)
    blocks = v.reshape(v.shape[:-1] + (-1, 32))
    amax = np.abs(blocks).max(-1, keepdims=True)
    byte = np.maximum(np.where(amax > 0, np.frexp(amax)[1] - 1 + 127, 0) - down, 1)
    scale = np.exp2(byte - 127.0)
    codes = (blocks / scale).astype(np.float32).astype(dtype).astype(np.float64)
    return np.moveaxis((codes * scale).reshape(v.shape), -1, axis)


WIDE = False


def mx_kscale(k):
    if not WIDE:
        return np.ones(k)
    levels = np.array([10, -10, 5, -5, 0])
    if k % 512:
        return np.exp2(np.random.permutation(np.resize(levels, k // 32))).repeat(32)
    a = np.empty((k // 512, 16))
    for p in range(k // 512):
        a[p, :8] = np.random.permutation(np.resize(levels, 8))
        for g in range(8):
            far = levels[np.abs(levels - a[p, g]) >= 10]
            a[p, g + 8] = far[np.random.randint(len(far))]
    return np.exp2(a.ravel()).repeat(32)


def f64(x):
    return np.asarray(x).astype(np.float64)


def striped(idx):
    return np.tile(idx.reshape(-1, 16).T, (8, 1)).astype(np.uint16)


def unstriped(offs):
    return offs[:16].T.reshape(-1).astype(np.int64)


E2M1 = np.array([0.0, 0.5, 1.0, 1.5, 2.0, 3.0, 4.0, 6.0, -0.0, -0.5, -1.0, -1.5, -2.0, -3.0, -4.0, -6.0])


def pack_weight(w, fmt):
    k, n = w.shape
    w = f64(np.asarray(w, np.float32).astype(ml_dtypes.bfloat16)).reshape(k // 32, 32, n)
    amax = np.abs(w).max(1)
    if fmt == "e4m3":
        byte = np.frexp(amax)[1] - 1 + 127 - 7
    else:
        mant, ex = np.frexp(amax / 6.0)
        byte = np.where(mant > 0.5, ex, ex - 1) + 127
    byte = np.clip(np.where(amax > 0, byte, 1), 1, 254)
    scaled = (w * np.exp2(127.0 - byte)[:, None, :]).reshape(k, n).astype(np.float32)
    by_word = np.ascontiguousarray(scaled.reshape(k // 512, 128, 4, n).transpose(0, 1, 3, 2))
    if fmt == "e4m3":
        words = by_word.astype(ml_dtypes.float8_e4m3fn).view(np.uint8)
    else:
        c = by_word.astype(ml_dtypes.float4_e2m1fn).view(np.uint8) & 0xF
        words = (c[..., 0::2] | (c[..., 1::2] << 4)).reshape(k // 512, 128, 2 * n)
    return np.ascontiguousarray(words), np.ascontiguousarray(byte.astype(np.uint8).reshape(k // 512, 16, n))


def unpack_weight(words, scales, fmt):
    g, _, n = scales.shape
    words = np.ascontiguousarray(words).reshape(g, 128, n, -1)
    if fmt == "e4m3":
        vals = words.view(ml_dtypes.float8_e4m3fn).astype(np.float64)
    else:
        nib = np.empty((g, 128, n, 4), np.uint8)
        nib[..., 0::2] = words & 0xF
        nib[..., 1::2] = words >> 4
        vals = E2M1[nib]
    vals = vals * np.repeat(np.exp2(scales.astype(np.float64) - 127.0), 8, axis=1)[..., None]
    return vals.transpose(0, 1, 3, 2).reshape(g * 512, n)


def silu(v):
    return v / (1.0 + np.exp(-np.maximum(v, -700.0)))


D, T, E, C, H, N, TOP = 2, 256, 6, 256, 512, 256, 3


def by_expert(wq, xq):
    return np.concatenate([wq[e].T @ xq[:, e * C:(e + 1) * C] for e in range(E)], axis=1)


def setup_inputs():
    n = np.random.standard_normal
    s = np.tile(mx_kscale(H), D)
    u = mx_kscale(H)
    X = D * T
    deal = np.repeat(np.arange(E), C).reshape(TOP, X)[:, np.random.permutation(X)]
    deal = np.take_along_axis(deal, np.argsort(np.random.rand(TOP, X), axis=0), axis=0)
    for _ in range(8):
        s_, t_ = np.random.permutation(X).reshape(2, -1); r = np.random.randint(TOP, size=X // 2); x, y = deal[r, s_].copy(), deal[r, t_].copy()
        ok = ~((deal[:, s_] == y).any(0) | (deal[:, t_] == x).any(0)); deal[r[ok], s_[ok]] = y[ok]; deal[r[ok], t_[ok]] = x[ok]
    order = np.lexsort((np.random.rand(TOP * X), deal.reshape(-1)))
    slot_sub = order % X; pos = np.empty(TOP * X, np.int64); pos[order] = np.arange(TOP * X); pos = pos.reshape(TOP, X)
    g = np.random.uniform(0.5, 1.5, (TOP, X)); g = g / g.sum(0)
    x = pack_weight(n((D * H, T)) * s[:, None], "e4m3")
    w = [pack_weight(m, "e2m1") for m in n((E, H, H)) / np.sqrt(H) / s[None, :H, None] * u]
    wm = pack_weight(n((D * H, N)) / np.sqrt(D * H) / np.tile(u, D)[:, None], "e4m3")
    return {
        "x_words": x[0],
        "x_scales": x[1],
        "w_words": np.stack([m[0] for m in w]),
        "w_scales": np.stack([m[1] for m in w]),
        "wm_words": wm[0],
        "wm_scales": wm[1],
        "gate": np.stack([np.tile(r, (128, 1)) for r in g]).astype(np.float32),
        "offs": striped(slot_sub),
        "pos1": striped(pos[0]),
        "pos2": striped(pos[1]),
        "pos3": striped(pos[2]),
    }


def reference(x_words, x_scales, w_words, w_scales, wm_words, wm_scales, gate, offs, pos1, pos2, pos3):
    w = np.stack([unpack_weight(w_words[e], w_scales[e], "e2m1") for e in range(E)])
    wm = unpack_weight(wm_words, wm_scales, "e4m3")
    idx = unstriped(offs)
    x = unpack_weight(x_words, x_scales, "e4m3")
    sub = x.reshape(D, H, T).transpose(1, 0, 2).reshape(H, D * T)
    y = silu(by_expert(w, sub[:, idx]))
    c = sum(f64(gate[r, :1]) * y[:, unstriped(p)] for r, p in enumerate((pos1, pos2, pos3)))
    cq = mxq(c, 0, "e4m3").reshape(H, D, T).transpose(1, 0, 2).reshape(D * H, T)
    return wm.T @ cq

from contextlib import ExitStack

import concourse.mybir as mybir
from concourse.masks import make_identity

FLOPS = 939524096

F32 = mybir.dt.float32
BF16 = mybir.dt.bfloat16
I32 = mybir.dt.int32
U32 = mybir.dt.uint32
U16 = mybir.dt.uint16
U8 = mybir.dt.uint8
FP8X4 = mybir.dt.float8_e4m3fn_x4
FP4X4 = mybir.dt.float4_e2m1fn_x4
MULT = mybir.AluOpType.mult
SILU = mybir.ActivationFunctionType.Silu

P = 128
HEADS, TOKENS, EXPERTS, CAP, H, N_OUT, TOP = 2, 256, 6, 256, 512, 256, 3
SUBS = HEADS * TOKENS
SLOTS = EXPERTS * CAP
ROW_BLOCKS = H // P
SUB_BLOCKS = SUBS // P
PER_COL = 16


def tile_moe_mhm_silu_kernel(
    tc, x_words, x_scales, w_words, w_scales, wm_words, wm_scales, gate, offs, pos1, pos2, pos3, out
):
    nc = tc.nc
    with ExitStack() as ctx:
        lists = ctx.enter_context(tc.tile_pool(name="lists", bufs=1))
        sb = ctx.enter_context(tc.tile_pool(name="sb", bufs=1))
        psum = ctx.enter_context(tc.psum_pool(name="psum", bufs=1))
        banks = [psum.tile([P, 512], F32, name=f"bank{b}") for b in range(8)]

        offs_t = lists.tile([P, SLOTS // PER_COL], U16, name="offs_t")
        pos_t = [lists.tile([P, SUBS // PER_COL], U16, name=f"pos_t{r}") for r in range(TOP)]

        xw = sb.tile([P, SUBS], I32, name="xw", tag="xw_then_gate", align_bytes=64)
        xs = sb.tile([P, SUBS], U8, name="xs", tag="xs_then_wm", align_bytes=64)
        ws = sb.tile([P, EXPERTS * H], U8, name="ws", align_bytes=64)
        wms = sb.tile([P, HEADS * N_OUT], U8, name="wms", align_bytes=64)
        ww = [sb.tile([P, 2 * 2 * H], U8, name=f"ww{i}", align_bytes=64) for i in range(EXPERTS // 2)]
        ident = sb.tile([P, P], F32, name="ident", align_bytes=64)

        for plane in (xs, ws, wms):
            nc.vector.memset(plane[:].bitcast(I32), 0)
        make_identity(nc, ident[:])

        def load_scale_rows(plane, rows):
            groups = rows.shape[0]
            by_j = rows.rearrange("g (q j) c -> j q g c", j=4)
            for j in range(4):
                nc.sync.dma_start(
                    out=plane[j:P:32, :].bitcast(I32).rearrange("q (g c) -> q g c", g=groups),
                    in_=by_j[j].bitcast(I32),
                )

        def load_w(i):
            nc.sync.dma_start(
                out=ww[i][:].bitcast(I32).rearrange("p (e b) -> p e b", e=2),
                in_=w_words[2 * i : 2 * i + 2, 0].rearrange("e p b -> p e b").bitcast(I32),
            )

        nc.sync.dma_start(offs_t[:], offs)
        nc.sync.dma_start(
            out=xw[:].rearrange("p (o t) -> p o t", o=HEADS),
            in_=x_words.rearrange("o p t d -> p o (t d)").bitcast(I32),
        )
        for tile, pos in zip(pos_t, (pos1, pos2, pos3)):
            nc.sync.dma_start(tile[:], pos)
        for i in range(EXPERTS // 2):
            load_w(i)
        load_scale_rows(xs, x_scales)
        load_scale_rows(ws, w_scales[:, 0])
        load_scale_rows(wms, wm_scales)

        xg = [sb.tile([P, CAP], U32, name=f"xg{e}", align_bytes=64) for e in range(EXPERTS)]
        sg = [sb.tile([P, CAP], U8, name=f"sg{e}", align_bytes=64) for e in range(EXPERTS)]
        y = [sb.tile([P, SLOTS], F32, name=f"y{t}", align_bytes=64) for t in range(ROW_BLOCKS)]

        def expert_product(e, t, dst):
            w0 = (e % 2) * 2 * H + t * 2 * P
            nc.tensor.matmul_mx(
                out=dst,
                lhsT=ww[e // 2][:, w0 : w0 + 2 * P].bitcast(FP4X4),
                lhsT_scale=ws[:, e * H + t * P : e * H + (t + 1) * P],
                rhs=xg[e][:].bitcast(FP8X4),
                rhs_scale=sg[e][:],
                start=True,
                stop=True,
            )

        def late_pair(e0, t, bank):
            for e in (e0, e0 + 1):
                expert_product(e, t, bank[:, (e - e0) * CAP : (e - e0 + 1) * CAP])
            nc.scalar.activation(out=y[t][:, e0 * CAP : (e0 + 2) * CAP], in_=bank[:], func=SILU)

        cols = CAP // PER_COL
        pieces = [offs_t[:, e * cols : (e + 1) * cols] for e in range(EXPERTS)]
        for e in range(EXPERTS):
            nc.vector.tensor_copy(out=xg[e][:], in_=xw[:].bitcast(U32).indirect(pieces[e]))
        gate_t = sb.tile([P, TOP, SUBS], F32, name="gate_t", tag="xw_then_gate", align_bytes=64)
        nc.sync.dma_start(out=gate_t[:], in_=gate.rearrange("r p z -> p r z"))
        for e in range(EXPERTS):
            nc.vector.tensor_copy(out=sg[e][:], in_=xs[:].indirect(pieces[e]))
            bank = banks[e % 4]
            expert_product(e, 0, bank[:, :CAP])
            nc.scalar.activation(out=y[0][:, e * CAP : (e + 1) * CAP], in_=bank[:, :CAP], func=SILU)
        wmw = sb.tile([P, HEADS * N_OUT], I32, name="wmw", tag="xs_then_wm", align_bytes=64)
        nc.sync.dma_start(
            out=wmw[:].rearrange("p (s n) -> p s n", s=HEADS),
            in_=wm_words.rearrange("s p n d -> p s (n d)").bitcast(I32),
        )
        later = [(t, e0) for t in range(1, ROW_BLOCKS) for e0 in range(0, EXPERTS, 2)]
        for i, (t, e0) in enumerate(later):
            late_pair(e0, t, banks[(i + 2) % 4])

        sums = banks[4:8]
        c_rows = [sb.tile([P, H], BF16, name=f"c_rows{b}", align_bytes=64) for b in range(SUB_BLOCKS)]

        def combine(t, blocks):
            z0, z1 = blocks[0] * P, (blocks[-1] + 1) * P
            for r in range(TOP):
                prod = sb.tile([P, z1 - z0], F32, name=f"prod{t}_{r}_{z0}", align_bytes=64)
                nc.vector.tensor_tensor(
                    out=prod[:],
                    in0=y[t][:].indirect(pos_t[r][:, z0 // PER_COL : z1 // PER_COL]),
                    in1=gate_t[:, r, z0:z1],
                    op=MULT,
                )
                for b in blocks:
                    nc.tensor.matmul(
                        out=sums[b][:, t * P : (t + 1) * P],
                        lhsT=prod[:, b * P - z0 : (b + 1) * P - z0],
                        rhs=ident[:],
                        is_transpose=True,
                        start=(r == 0),
                        stop=(r == TOP - 1),
                    )

        def round_rows(b, t0, t1):
            nc.scalar.copy(
                out=c_rows[b][:].rearrange("z (u p e) -> z u p e", u=2, e=2)[:, :, 32 * t0 : 32 * t1, :],
                in_=sums[b][:, t0 * P : t1 * P].rearrange("z (p u e) -> z u p e", u=2, e=2),
            )

        grouped = [sb.tile([P, 4 * P], BF16, name=f"grouped{b}", align_bytes=64) for b in range(SUB_BLOCKS)]
        c_codes = [sb.tile([P, P], U32, name=f"c_codes{b}", align_bytes=64) for b in range(SUB_BLOCKS)]
        c_scales = [sb.tile([P, P], U8, name=f"c_scales{b}", align_bytes=64) for b in range(SUB_BLOCKS)]

        def turn_back(b):
            pairs = c_rows[b][:].bitcast(F32)
            bank = banks[b % 2]
            for u in range(2):
                nc.tensor.transpose(bank[:, u * P : (u + 1) * P], pairs[:, u * P : (u + 1) * P], ident[:])
            nc.scalar.copy(
                out=grouped[b][:].bitcast(F32).rearrange("p (z u) -> p z u", u=2),
                in_=bank[:, : 2 * P].rearrange("p (u z) -> p z u", u=2),
            )

        def quantise(b):
            nc.vector.quantize_mx(out=c_codes[b][:].bitcast(FP8X4), scales=c_scales[b][:], in_=grouped[b][:])

        def merge_pass(b, nb, dst):
            o = b // 2
            cols_n = slice(o * N_OUT + nb * P, o * N_OUT + (nb + 1) * P)
            nc.tensor.matmul_mx(
                out=dst,
                lhsT=wmw[:, cols_n].bitcast(FP8X4),
                lhsT_scale=wms[:, cols_n],
                rhs=c_codes[b][:].bitcast(FP8X4),
                rhs_scale=c_scales[b][:],
                start=(o == 0),
                stop=(o == HEADS - 1),
            )

        every = list(range(SUB_BLOCKS))
        combine(0, every)
        combine(1, every)
        for b in every:
            round_rows(b, 0, 2)
        first, last = every[:-1], every[-1:]
        combine(2, first)
        combine(3, first)
        for b in first:
            round_rows(b, 2, 4)
        combine(2, last)
        round_rows(last[0], 2, 3)
        for b in first:
            turn_back(b)
        combine(3, last)
        round_rows(last[0], 3, 4)
        turn_back(last[0])
        for b in every:
            quantise(b)

        early = sb.tile([P, 2 * P], F32, name="early", align_bytes=64)
        for nb in range(2):
            for b in (0, 2):
                merge_pass(b, nb, banks[4][:, nb * P : (nb + 1) * P])
        nc.scalar.copy(out=early[:], in_=banks[4][:, : 2 * P])
        nc.sync.dma_start(
            out=out[:, :P].rearrange("(nb p) t -> p nb t", p=P),
            in_=early[:].rearrange("p (nb t) -> p nb t", nb=2),
        )
        late = [sb.tile([P, P], F32, name=f"late{nb}", align_bytes=64) for nb in range(2)]
        for b in (1, 3):
            for nb in range(2):
                merge_pass(b, nb, banks[2 + nb][:, :P])
        nc.vector.tensor_copy(out=late[0][:], in_=banks[2][:, :P])
        nc.sync.dma_start(out=out[:P, P:], in_=late[0][:])
        nc.scalar.copy(out=late[1][:], in_=banks[3][:, :P])
        nc.scalar.dma_start(out=out[P:, P:], in_=late[1][:])
